import numpy as np
import ml_dtypes


def mxq(x, axis, fmt="e4m3"):
    dtype, down = {"e4m3": (ml_dtypes.float8_e4m3fn, 7), "e5m2": (ml_dtypes.float8_e5m2, 14)}[fmt]
    v = np.moveaxis(np.asarray(x, np.float32).astype(ml_dtypes.bfloat16).astype(np.float64), axis, -1)
    blocks = v.reshape(v.shape[:-1] + (-1, 32))
    amax = np.abs(blocks).max(-1, keepdims=True)
    byte = np.maximum(np.where(amax > 0, np.frexp(amax)[1] - 1 + 127, 0) - down, 1)
    scale = np.exp2(byte - 127.0)
    codes = (blocks / scale).astype(np.float32).astype(dtype).astype(np.float64)
    return np.moveaxis((codes * scale).reshape(v.shape), -1, axis)


WIDE = False


def mx_kscale(k):
    if not WIDE:
        return np.ones(k)
    levels = np.array([10, -10, 5, -5, 0])
    if k % 512:
        return np.exp2(np.random.permutation(np.resize(levels, k // 32))).repeat(32)
    a = np.empty((k // 512, 16))
    for p in range(k // 512):
        a[p, :8] = np.random.permutation(np.resize(levels, 8))
        for g in range(8):
            far = levels[np.abs(levels - a[p, g]) >= 10]
            a[p, g + 8] = far[np.random.randint(len(far))]
    return np.exp2(a.ravel()).repeat(32)


def f64(x):
    return np.asarray(x).astype(np.float64)


def striped(idx):
    return np.tile(idx.reshape(-1, 16).T, (8, 1)).astype(np.uint16)


def unstriped(offs):
    return offs[:16].T.reshape(-1).astype(np.int64)


E2M1 = np.array([0.0, 0.5, 1.0, 1.5, 2.0, 3.0, 4.0, 6.0, -0.0, -0.5, -1.0, -1.5, -2.0, -3.0, -4.0, -6.0])


def pack_weight(w, fmt):
    k, n = w.shape
    w = f64(np.asarray(w, np.float32).astype(ml_dtypes.bfloat16)).reshape(k // 32, 32, n)
    amax = np.abs(w).max(1)
    if fmt == "e4m3":
        byte = np.frexp(amax)[1] - 1 + 127 - 7
    else:
        mant, ex = np.frexp(amax / 6.0)
        byte = np.where(mant > 0.5, ex, ex - 1) + 127
    byte = np.clip(np.where(amax > 0, byte, 1), 1, 254)
    scaled = (w * np.exp2(127.0 - byte)[:, None, :]).reshape(k, n).astype(np.float32)
    by_word = np.ascontiguousarray(scaled.reshape(k // 512, 128, 4, n).transpose(0, 1, 3, 2))
    if fmt == "e4m3":
        words = by_word.astype(ml_dtypes.float8_e4m3fn).view(np.uint8)
    else:
        c = by_word.astype(ml_dtypes.float4_e2m1fn).view(np.uint8) & 0xF
        words = (c[..., 0::2] | (c[..., 1::2] << 4)).reshape(k // 512, 128, 2 * n)
    return np.ascontiguousarray(words), np.ascontiguousarray(byte.astype(np.uint8).reshape(k // 512, 16, n))


def unpack_weight(words, scales, fmt):
    g, _, n = scales.shape
    words = np.ascontiguousarray(words).reshape(g, 128, n, -1)
    if fmt == "e4m3":
        vals = words.view(ml_dtypes.float8_e4m3fn).astype(np.float64)
    else:
        nib = np.empty((g, 128, n, 4), np.uint8)
        nib[..., 0::2] = words & 0xF
        nib[..., 1::2] = words >> 4
        vals = E2M1[nib]
    vals = vals * np.repeat(np.exp2(scales.astype(np.float64) - 127.0), 8, axis=1)[..., None]
    return vals.transpose(0, 1, 3, 2).reshape(g * 512, n)


def relu(v):
    return np.maximum(v, 0.0)


K, T, E, C, H, N = 1024, 640, 4, 128, 1024, 512
R = 4


def by_expert(wq, xq):
    return np.concatenate([wq[e].T @ xq[:, e * C:(e + 1) * C] for e in range(E)], axis=1)


def setup_inputs():
    n = np.random.standard_normal
    s = mx_kscale(K)[:, None]
    u = mx_kscale(H)
    slot_token = np.concatenate([r * (T // R) + np.random.permutation(T // R)[:C // R] for e in range(E) for r in range(R)])
    w1 = [pack_weight(m, "e2m1") for m in n((E, K, H)) / np.sqrt(K) / s[None] * u[None, None, :]]
    w2 = [pack_weight(m, "e2m1") for m in n((E, H, N)) / np.sqrt(H) / u[None, :, None]]
    x = pack_weight(n((K, T)) * s, "e4m3")
    return {
        "x_words": x[0],
        "x_scales": x[1],
        "w1_words": np.stack([m[0] for m in w1]),
        "w1_scales": np.stack([m[1] for m in w1]),
        "w2_words": np.stack([m[0] for m in w2]),
        "w2_scales": np.stack([m[1] for m in w2]),
        "offs": striped(slot_token),
    }


def reference(x_words, x_scales, w1_words, w1_scales, w2_words, w2_scales, offs):
    idx = unstriped(offs)
    w1 = np.stack([unpack_weight(w1_words[e], w1_scales[e], "e2m1") for e in range(E)])
    w2 = np.stack([unpack_weight(w2_words[e], w2_scales[e], "e2m1") for e in range(E)])
    xq = unpack_weight(x_words, x_scales, "e4m3")[:, idx]
    h = relu(by_expert(w1, xq))
    y = by_expert(w2, mxq(h, 0, "e4m3"))
    return y.reshape(N, E, R, C // R).transpose(0, 2, 1, 3).reshape(N, E * C)

from contextlib import ExitStack

import concourse.mybir as mybir
from concourse.masks import make_identity

K, T, E, C, H, N, R = 1024, 640, 4, 128, 1024, 512, 4
FLOPS = 2 * E * C * (K * H + H * N)

F32 = mybir.dt.float32
BF16 = mybir.dt.bfloat16
I32 = mybir.dt.int32
U32 = mybir.dt.uint32
U16 = mybir.dt.uint16
U8 = mybir.dt.uint8
FP8X4 = mybir.dt.float8_e4m3fn_x4
FP4X4 = mybir.dt.float4_e2m1fn_x4
RELU = mybir.ActivationFunctionType.Relu

P = 128
PASSES = 2
BANK = 512


def tile_moe_pke_mlp_relu_kernel(tc, x_words, x_scales, w1_words, w1_scales, w2_words, w2_scales, offs, out):
    nc = tc.nc
    with ExitStack() as ctx:
        keep = ctx.enter_context(tc.tile_pool(name="keep", bufs=1))
        psum = ctx.enter_context(tc.psum_pool(name="psum", bufs=8))

        offsets = keep.tile([P, E * C // 16], U16, name="offsets")
        xw = [keep.tile([P, T], I32, name=f"xw{o}", align_bytes=64) for o in range(PASSES)]
        xs = keep.tile([P, PASSES, T], U8, name="xs", align_bytes=64)
        w1 = [[keep.tile([P, 2 * H], U8, name=f"w1_{e}_{s}", align_bytes=64) for s in range(PASSES)] for e in range(1)]
        w1r = [keep.tile([P, PASSES, 2 * H], U8, name=f"w1r_{e}", align_bytes=64) for e in range(1, E)]
        w1s = [keep.tile([P, PASSES, H], U8, name=f"w1s_{e}", align_bytes=64) for e in range(E)]
        w2 = [keep.tile([P, PASSES, 2 * N], U8, name=f"w2_{e}", align_bytes=64) for e in range(E)]
        w2s = keep.tile([P, E * PASSES, N], U8, name="w2s", align_bytes=64)
        ident = keep.tile([P, P], F32, name="ident", align_bytes=64)
        stage = keep.tile([P, N // P, E * C], F32, name="stage", align_bytes=64)

        def w1_pass(e, s):
            return w1[0][s][:] if e == 0 else w1r[e - 1][:, s, :]

        def load_scales(plane, rows):
            for r in range(4):
                nc.sync.dma_start(plane[r:P:32, :, :].bitcast(I32), rows[r].bitcast(I32))

        nc.vector.memset(xs[:].rearrange("p o t -> p (o t)").bitcast(I32), 0)
        make_identity(nc, ident[:])

        nc.sync.dma_start(offsets[:], offs)
        nc.sync.dma_start(xw[0][:], x_words[0].rearrange("p t r -> p (t r)").bitcast(I32))
        load_scales(xs, x_scales.rearrange("o (q r) t -> r q o t", r=4))
        nc.sync.dma_start(w1[0][0][:].bitcast(I32), w1_words[0, 0].bitcast(I32))
        nc.sync.dma_start(xw[1][:], x_words[1].rearrange("p t r -> p (t r)").bitcast(I32))
        load_scales(w1s[0], w1_scales[0].rearrange("s (q r) n -> r q s n", r=4))
        nc.sync.dma_start(w1[0][1][:].bitcast(I32), w1_words[0, 1].bitcast(I32))
        for e in range(1, E):
            load_scales(w1s[e], w1_scales[e].rearrange("s (q r) n -> r q s n", r=4))
            nc.sync.dma_start(w1r[e - 1][:].bitcast(I32), w1_words[e].rearrange("s p b -> p s b").bitcast(I32))
        load_scales(w2s, w2_scales.rearrange("e s (q r) n -> r q (e s) n", r=4))
        for e in range(E):
            nc.sync.dma_start(w2[e][:].bitcast(I32), w2_words[e].rearrange("s p b -> p s b").bitcast(I32))

        gw, gs = {}, {}
        for first, count in ((0, 1), (1, 1), (2, 2)):
            cols = offsets[:, first * C // 16 : (first + count) * C // 16]
            for o in range(PASSES):
                words = keep.tile([P, count * C], U32, name=f"gw{first}_{o}", align_bytes=64)
                scales = keep.tile([P, count * C], U8, name=f"gs{first}_{o}", align_bytes=64)
                nc.vector.tensor_copy(words[:], xw[o][:].bitcast(U32).indirect(cols))
                nc.vector.tensor_copy(scales[:], xs[:, o, :].indirect(cols))
                for e in range(first, first + count):
                    c0 = (e - first) * C
                    gw[e, o] = words[:, c0 : c0 + C]
                    gs[e, o] = scales[:, c0 : c0 + C]

        hb = [keep.tile([P, PASSES, BANK], BF16, name=f"hb{e}", align_bytes=64) for e in range(E)]
        ht = [keep.tile([P, PASSES, BANK], BF16, name=f"ht{e}", align_bytes=64) for e in range(E)]
        hq = [keep.tile([P, PASSES, C], U32, name=f"hq{e}", align_bytes=64) for e in range(E)]
        hs = [keep.tile([P, PASSES, C], U8, name=f"hs{e}", align_bytes=64) for e in range(E)]

        def layer1(e):
            banks = [psum.tile([P, BANK], F32, name="bank", tag="bank") for g in range(PASSES)]
            steps = [(g, s) for g in range(PASSES) for s in range(PASSES)]
            if e == 0:
                steps = [(g, s) for s in range(PASSES) for g in range(PASSES)]
            for g, s in steps:
                nc.tensor.matmul_mx(
                    out=banks[g][:],
                    lhsT=gw[e, s].bitcast(FP8X4),
                    lhsT_scale=gs[e, s],
                    rhs=w1_pass(e, s)[:, 2 * BANK * g : 2 * BANK * (g + 1)].bitcast(FP4X4),
                    rhs_scale=w1s[e][:, s, BANK * g : BANK * (g + 1)],
                    start=(s == 0),
                    stop=(s == PASSES - 1),
                )
            for g in range(PASSES):
                nc.scalar.activation(
                    hb[e][:, g, :].rearrange("c (u p d) -> c u p d", u=2, d=2),
                    banks[g][:].rearrange("c (p u d) -> c u p d", u=2, d=2),
                    RELU,
                )

        def turn(e, groups, on_scalar):
            for gs_ in groups:
                n = len(gs_)
                g0 = gs_[0]
                bank = psum.tile([P, BANK], F32, name="bank", tag="bank")
                for g in gs_:
                    pairs = hb[e][:, g, :].bitcast(F32)
                    for u in range(2):
                        c0 = ((g - g0) * 2 + u) * C
                        nc.tensor.transpose(bank[:, c0 : c0 + C], pairs[:, u * P : (u + 1) * P], ident[:])
                dst = ht[e][:, g0 : g0 + n, :].bitcast(F32).rearrange("p g (c u) -> p g c u", u=2)
                src = bank[:, : n * 2 * C].rearrange("p (g u c) -> p g c u", u=2, c=C)
                if on_scalar:
                    nc.scalar.copy(dst, src)
                else:
                    nc.vector.tensor_copy(dst, src)
                nc.vector.quantize_mx(
                    out=hq[e][:, g0 : g0 + n, :].rearrange("p g c -> p (g c)").bitcast(FP8X4),
                    scales=hs[e][:, g0 : g0 + n, :].rearrange("p g c -> p (g c)"),
                    in_=ht[e][:, g0 : g0 + n, :].rearrange("p g c -> p (g c)"),
                )

        def product2(dst, e, j):
            for g in range(PASSES):
                nc.tensor.matmul_mx(
                    out=dst,
                    lhsT=w2[e][:, g, 2 * P * j : 2 * P * (j + 1)].bitcast(FP4X4),
                    lhsT_scale=w2s[:, e * PASSES + g, P * j : P * (j + 1)],
                    rhs=hq[e][:, g, :].bitcast(FP8X4),
                    rhs_scale=hs[e][:, g, :],
                    start=(g == 0),
                    stop=(g == PASSES - 1),
                )

        by_rank = stage[:].rearrange("p j (m e u) -> p j m e u", m=R, e=E)

        def layer2_expert(e, on_scalar):
            bank = psum.tile([P, BANK], F32, name="bank", tag="bank")
            for j in range(N // P):
                product2(bank[:, j * C : (j + 1) * C], e, j)
            dst = by_rank[:, :, :, e, :]
            src = bank[:].rearrange("p (j m u) -> p j m u", j=N // P, m=R)
            if on_scalar:
                nc.scalar.copy(dst, src)
            else:
                nc.vector.tensor_copy(dst, src)

        def layer2_rows(j, first, on_scalar):
            bank = psum.tile([P, BANK], F32, name="bank", tag="bank")
            for e in range(first, E):
                product2(bank[:, (e - first) * C : (e - first + 1) * C], e, j)
            dst = by_rank[:, j, :, first:, :]
            src = bank[:, : (E - first) * C].rearrange("p (e m u) -> p m e u", m=R, u=C // R)
            if on_scalar:
                nc.scalar.copy(dst, src)
            else:
                nc.vector.tensor_copy(dst, src)
            nc.sync.dma_start(out[j * P : (j + 1) * P, :], stage[:, j, :])

        layer1(0)
        layer1(1)
        turn(0, [[0, 1]], True)
        layer1(2)
        turn(1, [[0, 1]], True)
        layer1(3)
        turn(2, [[0, 1]], False)
        turn(3, [[0], [1]], False)
        layer2_expert(0, True)
        layer2_expert(1, True)
        for j in range(N // P):
            layer2_rows(j, 2, j % 2 == 1)
